import numpy as np
import ml_dtypes


def mxq(x, axis, fmt="e4m3"):
    dtype, down = {"e4m3": (ml_dtypes.float8_e4m3fn, 7), "e5m2": (ml_dtypes.float8_e5m2, 14)}[fmt]
    v = np.moveaxis(np.asarray(x, np.float32).astype(ml_dtypes.bfloat16).astype(np.float64), axis, -1)
    blocks = v.reshape(v.shape[:-1] + (-1, 32))
    amax = np.abs(blocks).max(-1, keepdims=True)
    byte = np.maximum(np.where(amax > 0, np.frexp(amax)[1] - 1 + 127, 0) - down, 1)
    scale = np.exp2(byte - 127.0)
    codes = (blocks / scale).astype(np.float32).astype(dtype).astype(np.float64)
    return np.moveaxis((codes * scale).reshape(v.shape), -1, axis)


WIDE = False


def mx_kscale(k):
    if not WIDE:
        return np.ones(k)
    levels = np.array([10, -10, 5, -5, 0])
    if k % 512:
        return np.exp2(np.random.permutation(np.resize(levels, k // 32))).repeat(32)
    a = np.empty((k // 512, 16))
    for p in range(k // 512):
        a[p, :8] = np.random.permutation(np.resize(levels, 8))
        for g in range(8):
            far = levels[np.abs(levels - a[p, g]) >= 10]
            a[p, g + 8] = far[np.random.randint(len(far))]
    return np.exp2(a.ravel()).repeat(32)


def f64(x):
    return np.asarray(x).astype(np.float64)


def striped(idx):
    return np.tile(idx.reshape(-1, 16).T, (8, 1)).astype(np.uint16)


def unstriped(offs):
    return offs[:16].T.reshape(-1).astype(np.int64)


def pack_weight(w):
    k, n = w.shape
    w = f64(np.asarray(w, np.float32).astype(ml_dtypes.bfloat16)).reshape(k // 32, 32, n)
    amax = np.abs(w).max(1)
    byte = np.clip(np.where(amax > 0, np.frexp(amax)[1] - 1 + 127 - 7, 1), 1, 254)
    scaled = (w * np.exp2(127.0 - byte)[:, None, :]).reshape(k, n).astype(np.float32)
    words = np.ascontiguousarray(scaled.reshape(k // 512, 128, 4, n).transpose(0, 1, 3, 2)).astype(ml_dtypes.float8_e4m3fn).view(np.uint8)
    return words, np.ascontiguousarray(byte.astype(np.uint8).reshape(k // 512, 16, n))


def unpack_weight(words, scales):
    g, p, n, _ = words.shape
    vals = np.ascontiguousarray(words).view(ml_dtypes.float8_e4m3fn).astype(np.float64) * np.repeat(np.exp2(scales.astype(np.float64) - 127.0), 8, axis=1)[..., None]
    return vals.transpose(0, 1, 3, 2).reshape(g * 512, n)


def silu(v):
    return v / (1.0 + np.exp(-np.maximum(v, -700.0)))


K, T, H, N, J, U = 1024, 512, 512, 256, 512, 1024


def setup_inputs():
    n = np.random.standard_normal
    s = mx_kscale(K)[:, None]
    u = mx_kscale(H)
    r = mx_kscale(J)[:, None]
    packed_xT = pack_weight(n((K, T)) * s)
    packed_w2 = pack_weight(n((H, N)) / np.sqrt(2 * H) / u[:, None])
    return {
        "x_words": packed_xT[0],
        "x_scales": packed_xT[1],
        "aT": (n((J, U)) * r).astype(np.float32),
        "w1": (n((K, H)) / np.sqrt(K) / s * u).astype(np.float32),
        "w3": (n((J, H)) / np.sqrt(J) / r).astype(np.float32),
        "w2_words": packed_w2[0],
        "w2_scales": packed_w2[1],
        "pos1": striped(np.random.permutation(T)),
        "pos2": striped(np.random.permutation(T)),
    }


def reference(x_words, x_scales, aT, w1, w3, w2_words, w2_scales, pos1, pos2):
    xq = unpack_weight(x_words, x_scales)
    h = silu(mxq(f64(w1), 0, "e4m3").T @ xq)
    f = mxq(f64(w3), 0, "e4m3").T @ mxq(f64(aT), 0, "e4m3")
    z = h[:, unstriped(pos1)] * f[:, :T] + h[:, unstriped(pos2)] * f[:, T:2 * T]
    return unpack_weight(w2_words, w2_scales).T @ mxq(z, 0, "e4m3")

@@ -1,0 +1,243 @@
+from contextlib import ExitStack
+
+import concourse.mybir as mybir
+from concourse.masks import make_identity
+
+K, T, H, N, J, U = 1024, 512, 512, 256, 512, 1024
+FLOPS = 2 * (K * H * T + J * H * U + H * N * T)
+
+F32 = mybir.dt.float32
+BF16 = mybir.dt.bfloat16
+U32 = mybir.dt.uint32
+I32 = mybir.dt.int32
+U16 = mybir.dt.uint16
+U8 = mybir.dt.uint8
+FP8X4 = mybir.dt.float8_e4m3fn_x4
+MULT = mybir.AluOpType.mult
+SILU = mybir.ActivationFunctionType.Silu
+
+P = 128
+HALF = 256
+
+
+def tile_picked_wdime_none_l_kernel(
+    tc, x_words, x_scales, aT, w1, w3, w2_words, w2_scales, pos1, pos2, out
+):
+    nc = tc.nc
+    with ExitStack() as ctx:
+        keep = ctx.enter_context(tc.tile_pool(name="keep", bufs=1))
+        psum = ctx.enter_context(tc.psum_pool(name="psum", bufs=1))
+
+        def copy_on(engine, dst, src):
+            if engine == "V":
+                nc.vector.tensor_copy(out=dst, in_=src)
+            else:
+                nc.scalar.copy(out=dst, in_=src)
+
+        def load_rows(name, rows):
+            raw = keep.tile([P, 4, HALF], F32, name=name, align_bytes=64)
+            nc.sync.dma_start(out=raw[:], in_=rows.rearrange("(p j) c -> p j c", j=4))
+            return raw
+
+        def cast_weight(name, raw, engine):
+            grouped = keep.tile([P, 4 * HALF], BF16, name=name, align_bytes=64)
+            copy_on(
+                engine,
+                grouped[:].rearrange("p (u r e j) -> p r j u e", u=2, e=2, j=4),
+                raw[:].rearrange("p j (r u e) -> p r j u e", u=2, e=2),
+            )
+            return grouped
+
+        def cast_plain(name, raw, engine):
+            grouped = keep.tile([P, 4 * HALF], BF16, name=name, align_bytes=64)
+            copy_on(
+                engine,
+                grouped[:].rearrange("p (c i j) -> p c j i", i=4, j=4),
+                raw[:].rearrange("p j (c i) -> p c j i", i=4),
+            )
+            return grouped
+
+        def quantise(name, grouped, width):
+            codes = keep.tile([P, width], U32, name=name + "_codes", align_bytes=64)
+            scales = keep.tile([P, width], U8, name=name + "_scales", align_bytes=64)
+            nc.vector.quantize_mx(out=codes[:].bitcast(FP8X4), scales=scales[:], in_=grouped)
+            return codes, scales
+
+        def mx(acc, lhs, lhs_scale, rhs, rhs_scale, start, stop):
+            nc.tensor.matmul_mx(
+                out=acc, lhsT=lhs.bitcast(FP8X4), lhsT_scale=lhs_scale,
+                rhs=rhs.bitcast(FP8X4), rhs_scale=rhs_scale, start=start, stop=stop,
+            )
+
+        x_plane = keep.tile([P, 2, T], U8, name="x_plane", align_bytes=64)
+        nc.vector.memset(x_plane[:].rearrange("p z c -> p (z c)").bitcast(U32), 0)
+        warm_in = keep.tile([P, 1], F32, name="warm_in")
+        warm_out = keep.tile([P, 1], F32, name="warm_out")
+        w2_plane = keep.tile([P, N], U8, name="w2_plane", align_bytes=64)
+        ident = keep.tile([P, P], F32, name="ident", align_bytes=64)
+        nc.gpsimd.memset(warm_in[:], 0.0)
+        nc.gpsimd.memset(w2_plane[:].bitcast(U32), 0)
+        make_identity(nc, ident[:])
+
+        for q in range(4):
+            nc.scalar.dma_start(
+                out=x_plane[32 * q : 32 * q + 4, :, :].bitcast(I32),
+                in_=x_scales[:, 4 * q : 4 * q + 4, :].rearrange("z r c -> r z c").bitcast(I32),
+            )
+        nc.scalar.activation(out=warm_out[:], in_=warm_in[:], func=SILU)
+
+        w1_raw = {}
+        w3_raw = {}
+        a_raw = {}
+        for z in range(2):
+            w1_raw[0, z] = load_rows("w1_raw0%d" % z, w1[512 * z : 512 * z + 512, 0:HALF])
+        x_codes = keep.tile([P, 2, T], U32, name="x_codes", align_bytes=64)
+        nc.sync.dma_start(
+            out=x_codes[:].bitcast(I32),
+            in_=x_words.rearrange("z p c r -> p z (c r)").bitcast(I32),
+        )
+        w3_raw[0] = load_rows("w3_raw0", w3[:, 0:HALF])
+        a_raw[0] = load_rows("a_raw0", aT[:, 0:HALF])
+        lists = []
+        for d, pos in enumerate((pos1, pos2)):
+            offsets = keep.tile([P, T // 16], U16, name="offsets%d" % d)
+            nc.sync.dma_start(offsets[:], pos)
+            lists.append(offsets)
+        a_raw[1] = load_rows("a_raw1", aT[:, HALF : 2 * HALF])
+        for z in range(2):
+            w1_raw[1, z] = load_rows("w1_raw1%d" % z, w1[512 * z : 512 * z + 512, HALF : 2 * HALF])
+        w3_raw[1] = load_rows("w3_raw1", w3[:, HALF : 2 * HALF])
+        for s in range(2, 4):
+            a_raw[s] = load_rows("a_raw%d" % s, aT[:, HALF * s : HALF * (s + 1)])
+        w2_codes = keep.tile([P, N], U32, name="w2_codes", align_bytes=64)
+        nc.sync.dma_start(
+            out=w2_codes[:].bitcast(I32), in_=w2_words[0].rearrange("p c r -> p (c r)").bitcast(I32)
+        )
+        for q in range(4):
+            nc.sync.dma_start(
+                out=w2_plane[32 * q : 32 * q + 4, :].bitcast(I32),
+                in_=w2_scales[0, 4 * q : 4 * q + 4, :].bitcast(I32),
+            )
+
+        w1_q = {}
+        w3_q = {}
+        a_q = {}
+        h = {}
+        f = {}
+        prod = {}
+
+        def make_w1(c, z, engine):
+            name = "w1_%d%d" % (c, z)
+            w1_q[c, z] = quantise(name, cast_weight(name, w1_raw[c, z], engine)[:], HALF)
+
+        def make_w3(c, engine):
+            name = "w3_%d" % c
+            w3_q[c] = quantise(name, cast_weight(name, w3_raw[c], engine)[:], HALF)
+
+        def make_a(s, engine):
+            name = "a_%d" % s
+            a_q[s] = quantise(name, cast_plain(name, a_raw[s], engine)[:], HALF)
+
+        def make_h(c):
+            for u in range(2):
+                acc = psum.tile([P, T], F32, name="acc", bufs=4)
+                cols = slice(P * u, P * (u + 1))
+                for z in range(2):
+                    codes, scales = w1_q[c, z]
+                    mx(acc[:], codes[:, cols], scales[:, cols], x_codes[:, z, :], x_plane[:, z, :], z == 0, z == 1)
+                h[c, u] = keep.tile([P, T], F32, name="h%d%d" % (c, u), align_bytes=64)
+                nc.scalar.activation(out=h[c, u][:], in_=acc[:], func=SILU)
+
+        def make_f(c, s):
+            acc = psum.tile([P, 2, HALF], F32, name="acc", bufs=4)
+            codes, scales = w3_q[c]
+            for u in range(2):
+                cols = slice(P * u, P * (u + 1))
+                mx(acc[:, u, :], codes[:, cols], scales[:, cols], a_q[s][0][:], a_q[s][1][:], True, True)
+            f[c, s] = keep.tile([P, 2, HALF], F32, name="f%d%d" % (c, s), align_bytes=64)
+            nc.scalar.copy(out=f[c, s][:], in_=acc[:])
+
+        def gather(c, u, s, lo, width):
+            d, first = s // 2, HALF * (s % 2) + lo
+            piece = keep.tile([P, width], F32, name="prod%d%d%d_%d" % (c, u, s, lo), align_bytes=64)
+            nc.vector.tensor_tensor(
+                piece[:],
+                h[c, u][:].indirect(lists[d][:, first // 16 : (first + width) // 16]),
+                f[c, s][:, u, lo : lo + width],
+                MULT,
+            )
+            for b in range(width // P):
+                prod[c, u, d, first // P + b] = piece[:, P * b : P * (b + 1)]
+
+        def turn(b):
+            zt_acc = psum.tile([P, 2, 2, P], F32, name="zt_acc", bufs=2)
+            for c in range(2):
+                for u in range(2):
+                    for d in range(2):
+                        nc.tensor.matmul(
+                            zt_acc[:, u, c, :], prod[c, u, d, b], ident[:], start=d == 0, stop=d == 1, is_transpose=True
+                        )
+            zt = keep.tile([P, H], BF16, name="zt%d" % b, align_bytes=64)
+            nc.scalar.copy(out=zt[:], in_=zt_acc[:].rearrange("p u c q -> p (u c q)"))
+            return zt
+
+        def finish(blocks, back_engine, out_engine):
+            width = P * len(blocks)
+            first = P * blocks[0]
+            back = psum.tile([P, 2, width], F32, name="back", bufs=2)
+            for n, b in enumerate(blocks):
+                words = turn(b)[:].bitcast(F32)
+                for u in range(2):
+                    nc.tensor.transpose(back[:, u, P * n : P * (n + 1)], words[:, P * u : P * (u + 1)], ident[:])
+            grouped = keep.tile([P, 4 * width], BF16, name="z_grouped%d" % first, align_bytes=64)
+            copy_on(
+                back_engine,
+                grouped[:].bitcast(F32).rearrange("p (v u) -> p v u", u=2),
+                back[:].rearrange("p u v -> p v u"),
+            )
+            codes, scales = quantise("z%d" % first, grouped[:], width)
+            acc = psum.tile([P, 2, width], F32, name="acc", bufs=4)
+            for m in range(2):
+                cols = slice(P * m, P * (m + 1))
+                mx(acc[:, m, :], w2_codes[:, cols], w2_plane[:, cols], codes[:], scales[:], True, True)
+            result = keep.tile([P, 2, width], F32, name="result%d" % first, align_bytes=64)
+            copy_on(out_engine, result[:], acc[:])
+            nc.sync.dma_start(
+                out=out[:, first : first + width].rearrange("(m p) v -> p m v", p=P), in_=result[:]
+            )
+
+        make_w1(0, 0, "V")
+        make_w1(0, 1, "V")
+        make_h(0)
+        make_w3(0, "V")
+        make_a(0, "V")
+        make_f(0, 0)
+        make_a(1, "S")
+        for u in range(2):
+            gather(0, u, 0, 0, HALF)
+        make_f(0, 1)
+        make_w1(1, 0, "V")
+        for u in range(2):
+            gather(0, u, 1, 0, HALF)
+        make_w1(1, 1, "V")
+        make_h(1)
+        make_w3(1, "S")
+        for s in range(2):
+            make_f(1, s)
+            for u in range(2):
+                gather(1, u, s, 0, HALF)
+        make_a(2, "S")
+        make_a(3, "S")
+        for c in range(2):
+            make_f(c, 2)
+            for u in range(2):
+                gather(c, u, 2, 0, HALF)
+        for c in range(2):
+            make_f(c, 3)
+        finish([0, 1], "S", "S")
+        for lo in (0, P):
+            for c in range(2):
+                for u in range(2):
+                    gather(c, u, 3, lo, P)
+        finish([2], "V", "S")
+        finish([3], "V", "S")

@@ -1,7 +1,6 @@
 from contextlib import ExitStack
 
 import concourse.mybir as mybir
-from concourse.masks import make_identity
 
 K, T, H, N, J, U = 1024, 512, 512, 256, 512, 1024
 FLOPS = 2 * (K * H * T + J * H * U + H * N * T)
@@ -14,10 +13,12 @@ U16 = mybir.dt.uint16
 U8 = mybir.dt.uint8
 FP8X4 = mybir.dt.float8_e4m3fn_x4
 MULT = mybir.AluOpType.mult
+ADD = mybir.AluOpType.add
 SILU = mybir.ActivationFunctionType.Silu
 
 P = 128
 HALF = 256
+SPARE = 192
 
 
 def tile_picked_wdime_none_l_kernel(
@@ -35,27 +36,13 @@ def tile_picked_wdime_none_l_kernel(
                 nc.scalar.copy(out=dst, in_=src)
 
         def load_rows(name, rows):
-            raw = keep.tile([P, 4, HALF], F32, name=name, align_bytes=64)
+            raw = keep.tile([P, 4, rows.shape[1]], F32, name=name, align_bytes=64)
             nc.sync.dma_start(out=raw[:], in_=rows.rearrange("(p j) c -> p j c", j=4))
             return raw
 
-        def cast_weight(name, raw, engine):
-            grouped = keep.tile([P, 4 * HALF], BF16, name=name, align_bytes=64)
-            copy_on(
-                engine,
-                grouped[:].rearrange("p (u r e j) -> p r j u e", u=2, e=2, j=4),
-                raw[:].rearrange("p j (r u e) -> p r j u e", u=2, e=2),
-            )
-            return grouped
-
-        def cast_plain(name, raw, engine):
-            grouped = keep.tile([P, 4 * HALF], BF16, name=name, align_bytes=64)
-            copy_on(
-                engine,
-                grouped[:].rearrange("p (c i j) -> p c j i", i=4, j=4),
-                raw[:].rearrange("p j (c i) -> p c j i", i=4),
-            )
-            return grouped
+        def cast_pair(dst, raw, a, engine):
+            src = raw.rearrange("p j (r t) -> p r j t", t=4)[:, :, :, 2 * a : 2 * a + 2]
+            copy_on(engine, dst.rearrange("p e r j -> p r j e"), src)
 
         def quantise(name, grouped, width):
             codes = keep.tile([P, width], U32, name=name + "_codes", align_bytes=64)
@@ -70,45 +57,40 @@ def tile_picked_wdime_none_l_kernel(
             )
 
         x_plane = keep.tile([P, 2, T], U8, name="x_plane", align_bytes=64)
-        nc.vector.memset(x_plane[:].rearrange("p z c -> p (z c)").bitcast(U32), 0)
-        warm_in = keep.tile([P, 1], F32, name="warm_in")
-        warm_out = keep.tile([P, 1], F32, name="warm_out")
+        nc.gpsimd.memset(x_plane[:].rearrange("p z c -> p (z c)").bitcast(U32), 0)
+        zeros = keep.tile([P, SPARE], F32, name="zeros")
+        h_all = keep.tile([P, 4 * T + SPARE], F32, name="h_all", align_bytes=64)
         w2_plane = keep.tile([P, N], U8, name="w2_plane", align_bytes=64)
-        ident = keep.tile([P, P], F32, name="ident", align_bytes=64)
-        nc.gpsimd.memset(warm_in[:], 0.0)
+        nc.gpsimd.memset(zeros[:], 0.0)
         nc.gpsimd.memset(w2_plane[:].bitcast(U32), 0)
-        make_identity(nc, ident[:])
 
         for q in range(4):
             nc.scalar.dma_start(
                 out=x_plane[32 * q : 32 * q + 4, :, :].bitcast(I32),
                 in_=x_scales[:, 4 * q : 4 * q + 4, :].rearrange("z r c -> r z c").bitcast(I32),
             )
-        nc.scalar.activation(out=warm_out[:], in_=warm_in[:], func=SILU)
+        nc.scalar.activation(out=h_all[:, 4 * T :], in_=zeros[:], func=SILU)
 
         w1_raw = {}
-        w3_raw = {}
-        a_raw = {}
+        x_codes = []
+        lists = []
+        a_raw = []
         for z in range(2):
             w1_raw[0, z] = load_rows("w1_raw0%d" % z, w1[512 * z : 512 * z + 512, 0:HALF])
-        x_codes = keep.tile([P, 2, T], U32, name="x_codes", align_bytes=64)
-        nc.sync.dma_start(
-            out=x_codes[:].bitcast(I32),
-            in_=x_words.rearrange("z p c r -> p z (c r)").bitcast(I32),
-        )
-        w3_raw[0] = load_rows("w3_raw0", w3[:, 0:HALF])
-        a_raw[0] = load_rows("a_raw0", aT[:, 0:HALF])
-        lists = []
-        for d, pos in enumerate((pos1, pos2)):
-            offsets = keep.tile([P, T // 16], U16, name="offsets%d" % d)
-            nc.sync.dma_start(offsets[:], pos)
-            lists.append(offsets)
-        a_raw[1] = load_rows("a_raw1", aT[:, HALF : 2 * HALF])
         for z in range(2):
+            words = keep.tile([P, T], U32, name="x_codes%d" % z, align_bytes=64)
+            nc.sync.dma_start(
+                out=words[:].bitcast(I32), in_=x_words[z].rearrange("p c r -> p (c r)").bitcast(I32)
+            )
+            x_codes.append(words)
+        for z in range(2):
+            offsets = keep.tile([P, T // 16], U16, name="offsets%d" % z)
+            nc.sync.dma_start(offsets[:], (pos1, pos2)[z])
+            lists.append(offsets)
             w1_raw[1, z] = load_rows("w1_raw1%d" % z, w1[512 * z : 512 * z + 512, HALF : 2 * HALF])
-        w3_raw[1] = load_rows("w3_raw1", w3[:, HALF : 2 * HALF])
-        for s in range(2, 4):
-            a_raw[s] = load_rows("a_raw%d" % s, aT[:, HALF * s : HALF * (s + 1)])
+        w3_raw = load_rows("w3_raw", w3)
+        for d in range(2):
+            a_raw.append(load_rows("a_raw%d" % d, aT[:, T * d : T * (d + 1)]))
         w2_codes = keep.tile([P, N], U32, name="w2_codes", align_bytes=64)
         nc.sync.dma_start(
             out=w2_codes[:].bitcast(I32), in_=w2_words[0].rearrange("p c r -> p (c r)").bitcast(I32)
@@ -119,125 +101,158 @@ def tile_picked_wdime_none_l_kernel(
                 in_=w2_scales[0, 4 * q : 4 * q + 4, :].bitcast(I32),
             )
 
-        w1_q = {}
+        pure_q = {}
+        mixed = {}
+        mixed_q = {}
         w3_q = {}
         a_q = {}
-        h = {}
-        f = {}
         prod = {}
+        grp = {}
+        picked = {}
+        staged = {}
+        h_acc = {}
+        f_acc = {}
 
-        def make_w1(c, z, engine):
-            name = "w1_%d%d" % (c, z)
-            w1_q[c, z] = quantise(name, cast_weight(name, w1_raw[c, z], engine)[:], HALF)
+        def make_pure(c, z, engine, tag):
+            grouped = keep.tile([P, 2, 64, 4], BF16, name="pure%d%d" % (c, z), tag=tag, align_bytes=64)
+            cast_pair(grouped[:], w1_raw[c, z][:], 0, engine)
+            pure_q[c, z] = quantise("pure%d%d" % (c, z), grouped[:].rearrange("p e r j -> p (e r j)"), P)
 
-        def make_w3(c, engine):
-            name = "w3_%d" % c
-            w3_q[c] = quantise(name, cast_weight(name, w3_raw[c], engine)[:], HALF)
+        def cast_mixed(c, z, engine):
+            if c == 0:
+                mixed[z] = keep.tile([P, 2, P, 4], BF16, name="mixed%d" % z, align_bytes=64)
+            cast_pair(mixed[z][:, :, 64 * c : 64 * c + 64, :], w1_raw[c, z][:], 1, engine)
 
-        def make_a(s, engine):
-            name = "a_%d" % s
-            a_q[s] = quantise(name, cast_plain(name, a_raw[s], engine)[:], HALF)
+        def quant_mixed(z):
+            mixed_q[z] = quantise("mixed%d" % z, mixed[z][:].rearrange("p e r j -> p (e r j)"), HALF)
 
-        def make_h(c):
-            for u in range(2):
-                acc = psum.tile([P, T], F32, name="acc", bufs=4)
-                cols = slice(P * u, P * (u + 1))
-                for z in range(2):
-                    codes, scales = w1_q[c, z]
-                    mx(acc[:], codes[:, cols], scales[:, cols], x_codes[:, z, :], x_plane[:, z, :], z == 0, z == 1)
-                h[c, u] = keep.tile([P, T], F32, name="h%d%d" % (c, u), align_bytes=64)
-                nc.scalar.activation(out=h[c, u][:], in_=acc[:], func=SILU)
+        def make_w3(a, engine):
+            grouped = picked[a][:, 2 * T : 3 * T].bitcast(BF16)
+            cast_pair(grouped.rearrange("p (e r j) -> p e r j", e=2, j=4), w3_raw[:], a, engine)
+            w3_q[a] = quantise("w3_%d" % a, grouped, HALF)
 
-        def make_f(c, s):
-            acc = psum.tile([P, 2, HALF], F32, name="acc", bufs=4)
-            codes, scales = w3_q[c]
-            for u in range(2):
-                cols = slice(P * u, P * (u + 1))
-                mx(acc[:, u, :], codes[:, cols], scales[:, cols], a_q[s][0][:], a_q[s][1][:], True, True)
-            f[c, s] = keep.tile([P, 2, HALF], F32, name="f%d%d" % (c, s), align_bytes=64)
-            nc.scalar.copy(out=f[c, s][:], in_=acc[:])
-
-        def gather(c, u, s, lo, width):
-            d, first = s // 2, HALF * (s % 2) + lo
-            piece = keep.tile([P, width], F32, name="prod%d%d%d_%d" % (c, u, s, lo), align_bytes=64)
-            nc.vector.tensor_tensor(
-                piece[:],
-                h[c, u][:].indirect(lists[d][:, first // 16 : (first + width) // 16]),
-                f[c, s][:, u, lo : lo + width],
-                MULT,
-            )
-            for b in range(width // P):
-                prod[c, u, d, first // P + b] = piece[:, P * b : P * (b + 1)]
-
-        def turn(b):
-            zt_acc = psum.tile([P, 2, 2, P], F32, name="zt_acc", bufs=2)
-            for c in range(2):
-                for u in range(2):
-                    for d in range(2):
-                        nc.tensor.matmul(
-                            zt_acc[:, u, c, :], prod[c, u, d, b], ident[:], start=d == 0, stop=d == 1, is_transpose=True
-                        )
-            zt = keep.tile([P, H], BF16, name="zt%d" % b, align_bytes=64)
-            nc.scalar.copy(out=zt[:], in_=zt_acc[:].rearrange("p u c q -> p (u c q)"))
-            return zt
-
-        def finish(blocks, back_engine, out_engine):
-            width = P * len(blocks)
-            first = P * blocks[0]
-            back = psum.tile([P, 2, width], F32, name="back", bufs=2)
-            for n, b in enumerate(blocks):
-                words = turn(b)[:].bitcast(F32)
-                for u in range(2):
-                    nc.tensor.transpose(back[:, u, P * n : P * (n + 1)], words[:, P * u : P * (u + 1)], ident[:])
-            grouped = keep.tile([P, 4 * width], BF16, name="z_grouped%d" % first, align_bytes=64)
+        def make_a(d, s, engine):
+            name = "a_%d%d" % (d, s)
+            if d == 0:
+                grouped = picked[s][:, 3 * T : 4 * T].bitcast(BF16)
+            else:
+                grouped = keep.tile([P, 4 * HALF], BF16, name=name, align_bytes=64)[:]
             copy_on(
-                back_engine,
-                grouped[:].bitcast(F32).rearrange("p (v u) -> p v u", u=2),
-                back[:].rearrange("p u v -> p v u"),
+                engine,
+                grouped.rearrange("p (c i j) -> p c j i", i=4, j=4),
+                a_raw[d][:, :, HALF * s : HALF * (s + 1)].rearrange("p j (c i) -> p c j i", i=4),
             )
-            codes, scales = quantise("z%d" % first, grouped[:], width)
-            acc = psum.tile([P, 2, width], F32, name="acc", bufs=4)
+            a_q[d, s] = quantise(name, grouped, HALF)
+
+        def make_h(n):
+            acc = psum.tile([P, T], F32, name="acc", bufs=6)
+            for z in range(2):
+                if n < 2:
+                    codes, scales = pure_q[n, z]
+                    cols = slice(0, P)
+                else:
+                    codes, scales = mixed_q[z]
+                    cols = slice(P * (n - 2), P * (n - 1))
+                mx(acc[:], codes[:, cols], scales[:, cols], x_codes[z][:], x_plane[:, z, :], z == 0, z == 1)
+            h_acc[n] = acc
+
+        def silu(n):
+            first = T * (3 - n)
+            nc.scalar.activation(out=h_all[:, first : first + T], in_=h_acc[n][:], func=SILU)
+
+        def gather(n, d, tag):
+            first = T * (3 - n)
+            if n == 0:
+                picked[d] = keep.tile([P, 4 * T], F32, name="picked%d" % d, tag=tag, align_bytes=64)
+            if n == 1:
+                staged[d] = keep.tile([P, T], F32, name="staged%d" % d, align_bytes=64)
+                dst = staged[d][:]
+            else:
+                dst = picked[d][:, T * n : T * (n + 1)]
+            nc.vector.tensor_copy(dst, h_all[:, first : first + T + SPARE].indirect(lists[d][:]))
+            if n == 0:
+                nc.sync.dma_start(out=picked[d][0:64, T : 2 * T], in_=picked[d][64:128, 0:T])
+            if n == 1:
+                nc.sync.dma_start(out=picked[d][64:128, T : 2 * T], in_=staged[d][64:128, :])
+                nc.sync.dma_start(out=picked[d][64:128, 0:T], in_=staged[d][0:64, :])
+
+        def filters(d, b):
+            acc = psum.tile([P, 4, P], F32, name="acc", bufs=6)
+            a_codes, a_scales = a_q[d, b // 2]
+            v_cols = slice(P * (b % 2), P * (b % 2 + 1))
+            for t in range(4):
+                codes, scales = w3_q[t // 2]
+                cols = slice(P * (t % 2), P * (t % 2 + 1))
+                mx(acc[:, t, :], codes[:, cols], scales[:, cols], a_codes[:, v_cols], a_scales[:, v_cols], True, True)
+            f_acc[d, b] = acc
+
+        def weigh(d, b):
+            prod[d, b] = keep.tile([P, 4, P], F32, name="prod%d%d" % (d, b), align_bytes=64)
+            columns = picked[d][:].rearrange("p (t v) -> p t v", t=4)[:, :, P * b : P * (b + 1)]
+            nc.vector.tensor_tensor(prod[d, b][:], f_acc[d, b][:], columns, MULT)
+
+        def add(b):
+            grp[b] = keep.tile([P, 4 * P], BF16, name="z_grouped%d" % b, align_bytes=64)
+            nc.vector.tensor_tensor(
+                grp[b][:].rearrange("p (c i t) -> p c t i", i=4, t=4),
+                prod[0, b][:].rearrange("p t (c i) -> p c t i", i=4),
+                prod[1, b][:].rearrange("p t (c i) -> p c t i", i=4),
+                ADD,
+            )
+
+        def project(b, engine):
+            codes, scales = quantise("z%d" % b, grp[b][:], P)
+            acc = psum.tile([P, 2, P], F32, name="out_acc", bufs=2)
             for m in range(2):
                 cols = slice(P * m, P * (m + 1))
                 mx(acc[:, m, :], w2_codes[:, cols], w2_plane[:, cols], codes[:], scales[:], True, True)
-            result = keep.tile([P, 2, width], F32, name="result%d" % first, align_bytes=64)
-            copy_on(out_engine, result[:], acc[:])
+            result = keep.tile([P, 2, P], F32, name="result%d" % b, align_bytes=64)
+            copy_on(engine, result[:], acc[:])
             nc.sync.dma_start(
-                out=out[:, first : first + width].rearrange("(m p) v -> p m v", p=P), in_=result[:]
+                out=out[:, P * b : P * (b + 1)].rearrange("(m p) v -> p m v", p=P), in_=result[:]
             )
 
-        make_w1(0, 0, "V")
-        make_w1(0, 1, "V")
+        make_pure(0, 0, "V", "pure00")
+        cast_mixed(0, 0, "S")
+        make_pure(0, 1, "V", "pure01")
+        cast_mixed(0, 1, "S")
         make_h(0)
-        make_w3(0, "V")
-        make_a(0, "V")
-        make_f(0, 0)
-        make_a(1, "S")
-        for u in range(2):
-            gather(0, u, 0, 0, HALF)
-        make_f(0, 1)
-        make_w1(1, 0, "V")
-        for u in range(2):
-            gather(0, u, 1, 0, HALF)
-        make_w1(1, 1, "V")
+        silu(0)
+        make_pure(1, 0, "V", "pure10")
+        gather(0, 0, "picked0")
+        make_pure(1, 1, "S", "late")
+        cast_mixed(1, 0, "S")
+        cast_mixed(1, 1, "S")
         make_h(1)
-        make_w3(1, "S")
+        silu(1)
+        gather(0, 1, "late")
+        for z in range(2):
+            quant_mixed(z)
+        for d in range(2):
+            gather(1, d, None)
+        for n in range(2, 4):
+            make_h(n)
+            silu(n)
+        for d in range(2):
+            make_w3(d, "S")
+            gather(2, d, None)
+        for d in range(2):
+            make_a(0, d, "S")
+            gather(3, d, None)
+        for b in range(4):
+            filters(0, b)
         for s in range(2):
-            make_f(1, s)
-            for u in range(2):
-                gather(1, u, s, 0, HALF)
-        make_a(2, "S")
-        make_a(3, "S")
-        for c in range(2):
-            make_f(c, 2)
-            for u in range(2):
-                gather(c, u, 2, 0, HALF)
-        for c in range(2):
-            make_f(c, 3)
-        finish([0, 1], "S", "S")
-        for lo in (0, P):
-            for c in range(2):
-                for u in range(2):
-                    gather(c, u, 3, lo, P)
-        finish([2], "V", "S")
-        finish([3], "V", "S")
+            make_a(1, s, "S")
+        weigh(0, 0)
+        filters(1, 0)
+        weigh(0, 1)
+        filters(1, 1)
+        for b in range(4):
+            weigh(1, b)
+            if b + 2 < 4:
+                weigh(0, b + 2)
+                filters(1, b + 2)
+            if b > 0:
+                project(b - 1, "S")
+            add(b)
+        project(3, "S")

@@ -64,19 +64,19 @@ def tile_picked_wdime_none_l_kernel(
         nc.gpsimd.memset(zeros[:], 0.0)
         nc.gpsimd.memset(w2_plane[:].bitcast(U32), 0)
 
-        for q in range(4):
-            nc.scalar.dma_start(
-                out=x_plane[32 * q : 32 * q + 4, :, :].bitcast(I32),
-                in_=x_scales[:, 4 * q : 4 * q + 4, :].rearrange("z r c -> r z c").bitcast(I32),
-            )
         nc.scalar.activation(out=h_all[:, 4 * T :], in_=zeros[:], func=SILU)
 
         w1_raw = {}
         x_codes = []
         lists = []
         a_raw = []
-        for z in range(2):
-            w1_raw[0, z] = load_rows("w1_raw0%d" % z, w1[512 * z : 512 * z + 512, 0:HALF])
+        w1_raw[0, 0] = load_rows("w1_raw00", w1[0:512, 0:HALF])
+        for q in range(4):
+            nc.sync.dma_start(
+                out=x_plane[32 * q : 32 * q + 4, :, :].bitcast(I32),
+                in_=x_scales[:, 4 * q : 4 * q + 4, :].rearrange("z r c -> r z c").bitcast(I32),
+            )
+        w1_raw[0, 1] = load_rows("w1_raw01", w1[512:1024, 0:HALF])
         for z in range(2):
             words = keep.tile([P, T], U32, name="x_codes%d" % z, align_bytes=64)
             nc.sync.dma_start(
@@ -136,7 +136,7 @@ def tile_picked_wdime_none_l_kernel(
             if d == 0:
                 grouped = picked[s][:, 3 * T : 4 * T].bitcast(BF16)
             else:
-                grouped = keep.tile([P, 4 * HALF], BF16, name=name, align_bytes=64)[:]
+                grouped = keep.tile([P, 4 * HALF], BF16, name=name, tag=name, align_bytes=64)[:]
             copy_on(
                 engine,
                 grouped.rearrange("p (c i j) -> p c j i", i=4, j=4),
@@ -144,8 +144,18 @@ def tile_picked_wdime_none_l_kernel(
             )
             a_q[d, s] = quantise(name, grouped, HALF)
 
+        def first_h():
+            for s in range(2):
+                acc = psum.tile([P, HALF], F32, name="acc", bufs=5)
+                cols = slice(HALF * s, HALF * (s + 1))
+                for z in range(2):
+                    codes, scales = pure_q[0, z]
+                    mx(acc[:], codes[:], scales[:], x_codes[z][:, cols], x_plane[:, z, cols], z == 0, z == 1)
+                first = 3 * T + HALF * s
+                nc.scalar.activation(out=h_all[:, first : first + HALF], in_=acc[:], func=SILU)
+
         def make_h(n):
-            acc = psum.tile([P, T], F32, name="acc", bufs=6)
+            acc = psum.tile([P, T], F32, name="acc", bufs=5)
             for z in range(2):
                 if n < 2:
                     codes, scales = pure_q[n, z]
@@ -177,7 +187,7 @@ def tile_picked_wdime_none_l_kernel(
                 nc.sync.dma_start(out=picked[d][64:128, 0:T], in_=staged[d][0:64, :])
 
         def filters(d, b):
-            acc = psum.tile([P, 4, P], F32, name="acc", bufs=6)
+            acc = psum.tile([P, 4, P], F32, name="acc", bufs=5)
             a_codes, a_scales = a_q[d, b // 2]
             v_cols = slice(P * (b % 2), P * (b % 2 + 1))
             for t in range(4):
@@ -186,38 +196,49 @@ def tile_picked_wdime_none_l_kernel(
                 mx(acc[:, t, :], codes[:, cols], scales[:, cols], a_codes[:, v_cols], a_scales[:, v_cols], True, True)
             f_acc[d, b] = acc
 
-        def weigh(d, b):
-            prod[d, b] = keep.tile([P, 4, P], F32, name="prod%d%d" % (d, b), align_bytes=64)
-            columns = picked[d][:].rearrange("p (t v) -> p t v", t=4)[:, :, P * b : P * (b + 1)]
-            nc.vector.tensor_tensor(prod[d, b][:], f_acc[d, b][:], columns, MULT)
+        def weigh(d, piece):
+            first, width = piece
+            prod[d, first] = keep.tile([P, 4, width], F32, name="prod%d_%d" % (d, first), align_bytes=64)
+            columns = picked[d][:].rearrange("p (t v) -> p t v", t=4)[:, :, first : first + width]
+            lo = first % P
+            nc.vector.tensor_tensor(prod[d, first][:], f_acc[d, first // P][:, :, lo : lo + width], columns, MULT)
 
-        def add(b):
-            grp[b] = keep.tile([P, 4 * P], BF16, name="z_grouped%d" % b, align_bytes=64)
+        def weigh_aside(b, tag):
+            filt = keep.tile([P, 4, P], F32, name="filt%d" % b, align_bytes=64)
+            nc.scalar.copy(out=filt[:], in_=f_acc[0, b][:])
+            prod[0, P * b] = keep.tile([P, 4, P], F32, name="prod0_%d" % (P * b), tag=tag, align_bytes=64)
+            columns = picked[0][:].rearrange("p (t v) -> p t v", t=4)[:, :, P * b : P * (b + 1)]
+            nc.gpsimd.tensor_tensor(prod[0, P * b][:], filt[:], columns, MULT)
+
+        def add(piece):
+            first, width = piece
+            grp[first] = keep.tile([P, 4 * width], BF16, name="z_grouped%d" % first, align_bytes=64)
             nc.vector.tensor_tensor(
-                grp[b][:].rearrange("p (c i t) -> p c t i", i=4, t=4),
-                prod[0, b][:].rearrange("p t (c i) -> p c t i", i=4),
-                prod[1, b][:].rearrange("p t (c i) -> p c t i", i=4),
+                grp[first][:].rearrange("p (c i t) -> p c t i", i=2, t=4),
+                prod[0, first - first % P][:, :, first % P : first % P + width].rearrange("p t (c i) -> p c t i", i=2),
+                prod[1, first - first % P][:, :, first % P : first % P + width].rearrange("p t (c i) -> p c t i", i=2),
                 ADD,
             )
 
-        def project(b, engine):
-            codes, scales = quantise("z%d" % b, grp[b][:], P)
-            acc = psum.tile([P, 2, P], F32, name="out_acc", bufs=2)
+        def project(piece):
+            first, width = piece
+            codes, scales = quantise("z%d" % first, grp[first][:], width)
+            acc = psum.tile([P, 2, width], F32, name="out_acc", bufs=3)
             for m in range(2):
                 cols = slice(P * m, P * (m + 1))
                 mx(acc[:, m, :], w2_codes[:, cols], w2_plane[:, cols], codes[:], scales[:], True, True)
-            result = keep.tile([P, 2, P], F32, name="result%d" % b, align_bytes=64)
-            copy_on(engine, result[:], acc[:])
-            nc.sync.dma_start(
-                out=out[:, P * b : P * (b + 1)].rearrange("(m p) v -> p m v", p=P), in_=result[:]
+            result = keep.tile([P, 2, width], F32, name="result%d" % first, align_bytes=64)
+            nc.scalar.copy(out=result[:], in_=acc[:])
+            queue = nc.scalar if first + width == T else nc.sync
+            queue.dma_start(
+                out=out[:, first : first + width].rearrange("(m p) v -> p m v", p=P), in_=result[:]
             )
 
         make_pure(0, 0, "V", "pure00")
         cast_mixed(0, 0, "S")
         make_pure(0, 1, "V", "pure01")
         cast_mixed(0, 1, "S")
-        make_h(0)
-        silu(0)
+        first_h()
         make_pure(1, 0, "V", "pure10")
         gather(0, 0, "picked0")
         make_pure(1, 1, "S", "late")
@@ -230,11 +251,11 @@ def tile_picked_wdime_none_l_kernel(
             quant_mixed(z)
         for d in range(2):
             gather(1, d, None)
-        for n in range(2, 4):
-            make_h(n)
-            silu(n)
+        for a in range(2):
+            make_w3(a, "S")
+            make_h(2 + a)
+            silu(2 + a)
         for d in range(2):
-            make_w3(d, "S")
             gather(2, d, None)
         for d in range(2):
             make_a(0, d, "S")
@@ -243,16 +264,18 @@ def tile_picked_wdime_none_l_kernel(
             filters(0, b)
         for s in range(2):
             make_a(1, s, "S")
-        weigh(0, 0)
-        filters(1, 0)
-        weigh(0, 1)
-        filters(1, 1)
+        pieces = [(0, 128), (128, 128), (256, 128), (384, 64), (448, 64)]
+        for b in range(2):
+            weigh(0, (P * b, P))
+            filters(1, b)
+        weigh_aside(2, "a_11")
+        weigh_aside(3, "prod0_3")
+        for b in range(2, 4):
+            filters(1, b)
         for b in range(4):
-            weigh(1, b)
-            if b + 2 < 4:
-                weigh(0, b + 2)
-                filters(1, b + 2)
-            if b > 0:
-                project(b - 1, "S")
-            add(b)
-        project(3, "S")
+            weigh(1, (P * b, P))
+        add(pieces[0])
+        for n, piece in enumerate(pieces):
+            if n + 1 < len(pieces):
+                add(pieces[n + 1])
+            project(piece)

from contextlib import ExitStack

import concourse.mybir as mybir

K, T, H, N, J, U = 1024, 512, 512, 256, 512, 1024
FLOPS = 2 * (K * H * T + J * H * U + H * N * T)

F32 = mybir.dt.float32
BF16 = mybir.dt.bfloat16
U32 = mybir.dt.uint32
I32 = mybir.dt.int32
U16 = mybir.dt.uint16
U8 = mybir.dt.uint8
FP8X4 = mybir.dt.float8_e4m3fn_x4
MULT = mybir.AluOpType.mult
ADD = mybir.AluOpType.add
SILU = mybir.ActivationFunctionType.Silu

P = 128
HALF = 256
SPARE = 192


def tile_picked_wdime_none_l_kernel(
    tc, x_words, x_scales, aT, w1, w3, w2_words, w2_scales, pos1, pos2, out
):
    nc = tc.nc
    with ExitStack() as ctx:
        keep = ctx.enter_context(tc.tile_pool(name="keep", bufs=1))
        psum = ctx.enter_context(tc.psum_pool(name="psum", bufs=1))

        def copy_on(engine, dst, src):
            if engine == "V":
                nc.vector.tensor_copy(out=dst, in_=src)
            else:
                nc.scalar.copy(out=dst, in_=src)

        def load_rows(name, rows):
            raw = keep.tile([P, 4, rows.shape[1]], F32, name=name, align_bytes=64)
            nc.sync.dma_start(out=raw[:], in_=rows.rearrange("(p j) c -> p j c", j=4))
            return raw

        def cast_pair(dst, raw, a, engine):
            src = raw.rearrange("p j (r t) -> p r j t", t=4)[:, :, :, 2 * a : 2 * a + 2]
            copy_on(engine, dst.rearrange("p e r j -> p r j e"), src)

        def quantise(name, grouped, width):
            codes = keep.tile([P, width], U32, name=name + "_codes", align_bytes=64)
            scales = keep.tile([P, width], U8, name=name + "_scales", align_bytes=64)
            nc.vector.quantize_mx(out=codes[:].bitcast(FP8X4), scales=scales[:], in_=grouped)
            return codes, scales

        def mx(acc, lhs, lhs_scale, rhs, rhs_scale, start, stop):
            nc.tensor.matmul_mx(
                out=acc, lhsT=lhs.bitcast(FP8X4), lhsT_scale=lhs_scale,
                rhs=rhs.bitcast(FP8X4), rhs_scale=rhs_scale, start=start, stop=stop,
            )

        x_plane = keep.tile([P, 2, T], U8, name="x_plane", align_bytes=64)
        nc.gpsimd.memset(x_plane[:].rearrange("p z c -> p (z c)").bitcast(U32), 0)
        zeros = keep.tile([P, SPARE], F32, name="zeros")
        h_all = keep.tile([P, 4 * T + SPARE], F32, name="h_all", align_bytes=64)
        w2_plane = keep.tile([P, N], U8, name="w2_plane", align_bytes=64)
        nc.gpsimd.memset(zeros[:], 0.0)
        nc.gpsimd.memset(w2_plane[:].bitcast(U32), 0)

        nc.scalar.activation(out=h_all[:, 4 * T :], in_=zeros[:], func=SILU)

        w1_raw = {}
        x_codes = []
        lists = []
        a_raw = []
        w1_raw[0, 0] = load_rows("w1_raw00", w1[0:512, 0:HALF])
        for q in range(4):
            nc.sync.dma_start(
                out=x_plane[32 * q : 32 * q + 4, :, :].bitcast(I32),
                in_=x_scales[:, 4 * q : 4 * q + 4, :].rearrange("z r c -> r z c").bitcast(I32),
            )
        w1_raw[0, 1] = load_rows("w1_raw01", w1[512:1024, 0:HALF])
        for z in range(2):
            words = keep.tile([P, T], U32, name="x_codes%d" % z, align_bytes=64)
            nc.sync.dma_start(
                out=words[:].bitcast(I32), in_=x_words[z].rearrange("p c r -> p (c r)").bitcast(I32)
            )
            x_codes.append(words)
        for z in range(2):
            offsets = keep.tile([P, T // 16], U16, name="offsets%d" % z)
            nc.sync.dma_start(offsets[:], (pos1, pos2)[z])
            lists.append(offsets)
            w1_raw[1, z] = load_rows("w1_raw1%d" % z, w1[512 * z : 512 * z + 512, HALF : 2 * HALF])
        w3_raw = load_rows("w3_raw", w3)
        for d in range(2):
            a_raw.append(load_rows("a_raw%d" % d, aT[:, T * d : T * (d + 1)]))
        w2_codes = keep.tile([P, N], U32, name="w2_codes", align_bytes=64)
        nc.sync.dma_start(
            out=w2_codes[:].bitcast(I32), in_=w2_words[0].rearrange("p c r -> p (c r)").bitcast(I32)
        )
        for q in range(4):
            nc.sync.dma_start(
                out=w2_plane[32 * q : 32 * q + 4, :].bitcast(I32),
                in_=w2_scales[0, 4 * q : 4 * q + 4, :].bitcast(I32),
            )

        pure_q = {}
        mixed = {}
        mixed_q = {}
        w3_q = {}
        a_q = {}
        prod = {}
        grp = {}
        picked = {}
        staged = {}
        h_acc = {}
        f_acc = {}

        def make_pure(c, z, engine, tag):
            grouped = keep.tile([P, 2, 64, 4], BF16, name="pure%d%d" % (c, z), tag=tag, align_bytes=64)
            cast_pair(grouped[:], w1_raw[c, z][:], 0, engine)
            pure_q[c, z] = quantise("pure%d%d" % (c, z), grouped[:].rearrange("p e r j -> p (e r j)"), P)

        def cast_mixed(c, z, engine):
            if c == 0:
                mixed[z] = keep.tile([P, 2, P, 4], BF16, name="mixed%d" % z, align_bytes=64)
            cast_pair(mixed[z][:, :, 64 * c : 64 * c + 64, :], w1_raw[c, z][:], 1, engine)

        def quant_mixed(z):
            mixed_q[z] = quantise("mixed%d" % z, mixed[z][:].rearrange("p e r j -> p (e r j)"), HALF)

        def make_w3(a, engine):
            grouped = picked[a][:, 2 * T : 3 * T].bitcast(BF16)
            cast_pair(grouped.rearrange("p (e r j) -> p e r j", e=2, j=4), w3_raw[:], a, engine)
            w3_q[a] = quantise("w3_%d" % a, grouped, HALF)

        def make_a(d, s, engine):
            name = "a_%d%d" % (d, s)
            if d == 0:
                grouped = picked[s][:, 3 * T : 4 * T].bitcast(BF16)
            else:
                grouped = keep.tile([P, 4 * HALF], BF16, name=name, tag=name, align_bytes=64)[:]
            copy_on(
                engine,
                grouped.rearrange("p (c i j) -> p c j i", i=4, j=4),
                a_raw[d][:, :, HALF * s : HALF * (s + 1)].rearrange("p j (c i) -> p c j i", i=4),
            )
            a_q[d, s] = quantise(name, grouped, HALF)

        def first_h():
            for s in range(2):
                acc = psum.tile([P, HALF], F32, name="acc", bufs=5)
                cols = slice(HALF * s, HALF * (s + 1))
                for z in range(2):
                    codes, scales = pure_q[0, z]
                    mx(acc[:], codes[:], scales[:], x_codes[z][:, cols], x_plane[:, z, cols], z == 0, z == 1)
                first = 3 * T + HALF * s
                nc.scalar.activation(out=h_all[:, first : first + HALF], in_=acc[:], func=SILU)

        def make_h(n):
            acc = psum.tile([P, T], F32, name="acc", bufs=5)
            for z in range(2):
                if n < 2:
                    codes, scales = pure_q[n, z]
                    cols = slice(0, P)
                else:
                    codes, scales = mixed_q[z]
                    cols = slice(P * (n - 2), P * (n - 1))
                mx(acc[:], codes[:, cols], scales[:, cols], x_codes[z][:], x_plane[:, z, :], z == 0, z == 1)
            h_acc[n] = acc

        def silu(n):
            first = T * (3 - n)
            nc.scalar.activation(out=h_all[:, first : first + T], in_=h_acc[n][:], func=SILU)

        def gather(n, d, tag):
            first = T * (3 - n)
            if n == 0:
                picked[d] = keep.tile([P, 4 * T], F32, name="picked%d" % d, tag=tag, align_bytes=64)
            if n == 1:
                staged[d] = keep.tile([P, T], F32, name="staged%d" % d, align_bytes=64)
                dst = staged[d][:]
            else:
                dst = picked[d][:, T * n : T * (n + 1)]
            nc.vector.tensor_copy(dst, h_all[:, first : first + T + SPARE].indirect(lists[d][:]))
            if n == 0:
                nc.sync.dma_start(out=picked[d][0:64, T : 2 * T], in_=picked[d][64:128, 0:T])
            if n == 1:
                nc.sync.dma_start(out=picked[d][64:128, T : 2 * T], in_=staged[d][64:128, :])
                nc.sync.dma_start(out=picked[d][64:128, 0:T], in_=staged[d][0:64, :])

        def filters(d, b):
            acc = psum.tile([P, 4, P], F32, name="acc", bufs=5)
            a_codes, a_scales = a_q[d, b // 2]
            v_cols = slice(P * (b % 2), P * (b % 2 + 1))
            for t in range(4):
                codes, scales = w3_q[t // 2]
                cols = slice(P * (t % 2), P * (t % 2 + 1))
                mx(acc[:, t, :], codes[:, cols], scales[:, cols], a_codes[:, v_cols], a_scales[:, v_cols], True, True)
            f_acc[d, b] = acc

        def weigh(d, piece):
            first, width = piece
            prod[d, first] = keep.tile([P, 4, width], F32, name="prod%d_%d" % (d, first), align_bytes=64)
            columns = picked[d][:].rearrange("p (t v) -> p t v", t=4)[:, :, first : first + width]
            lo = first % P
            nc.vector.tensor_tensor(prod[d, first][:], f_acc[d, first // P][:, :, lo : lo + width], columns, MULT)

        def weigh_aside(b, tag):
            filt = keep.tile([P, 4, P], F32, name="filt%d" % b, align_bytes=64)
            nc.scalar.copy(out=filt[:], in_=f_acc[0, b][:])
            prod[0, P * b] = keep.tile([P, 4, P], F32, name="prod0_%d" % (P * b), tag=tag, align_bytes=64)
            columns = picked[0][:].rearrange("p (t v) -> p t v", t=4)[:, :, P * b : P * (b + 1)]
            nc.gpsimd.tensor_tensor(prod[0, P * b][:], filt[:], columns, MULT)

        def add(piece):
            first, width = piece
            grp[first] = keep.tile([P, 4 * width], BF16, name="z_grouped%d" % first, align_bytes=64)
            nc.vector.tensor_tensor(
                grp[first][:].rearrange("p (c i t) -> p c t i", i=2, t=4),
                prod[0, first - first % P][:, :, first % P : first % P + width].rearrange("p t (c i) -> p c t i", i=2),
                prod[1, first - first % P][:, :, first % P : first % P + width].rearrange("p t (c i) -> p c t i", i=2),
                ADD,
            )

        def project(piece):
            first, width = piece
            codes, scales = quantise("z%d" % first, grp[first][:], width)
            acc = psum.tile([P, 2, width], F32, name="out_acc", bufs=3)
            for m in range(2):
                cols = slice(P * m, P * (m + 1))
                mx(acc[:, m, :], w2_codes[:, cols], w2_plane[:, cols], codes[:], scales[:], True, True)
            result = keep.tile([P, 2, width], F32, name="result%d" % first, align_bytes=64)
            nc.scalar.copy(out=result[:], in_=acc[:])
            queue = nc.scalar if first + width == T else nc.sync
            queue.dma_start(
                out=out[:, first : first + width].rearrange("(m p) v -> p m v", p=P), in_=result[:]
            )

        make_pure(0, 0, "V", "pure00")
        cast_mixed(0, 0, "S")
        make_pure(0, 1, "V", "pure01")
        cast_mixed(0, 1, "S")
        first_h()
        make_pure(1, 0, "V", "pure10")
        gather(0, 0, "picked0")
        make_pure(1, 1, "S", "late")
        cast_mixed(1, 0, "S")
        cast_mixed(1, 1, "S")
        make_h(1)
        silu(1)
        gather(0, 1, "late")
        for z in range(2):
            quant_mixed(z)
        for d in range(2):
            gather(1, d, None)
        for a in range(2):
            make_w3(a, "S")
            make_h(2 + a)
            silu(2 + a)
        for d in range(2):
            gather(2, d, None)
        for d in range(2):
            make_a(0, d, "S")
            gather(3, d, None)
        for b in range(4):
            filters(0, b)
        for s in range(2):
            make_a(1, s, "S")
        pieces = [(0, 128), (128, 128), (256, 128), (384, 64), (448, 64)]
        for b in range(2):
            weigh(0, (P * b, P))
            filters(1, b)
        weigh_aside(2, "a_11")
        weigh_aside(3, "prod0_3")
        for b in range(2, 4):
            filters(1, b)
        for b in range(4):
            weigh(1, (P * b, P))
        add(pieces[0])
        for n, piece in enumerate(pieces):
            if n + 1 < len(pieces):
                add(pieces[n + 1])
            project(piece)
